import numpy as np, ml_dtypes
CORES = [16,18,20,22]
N = 4
BF = ml_dtypes.bfloat16
V, S, P, Q = 3, 1024, 128, 256
def fill(rng, l, cap):
    l = np.minimum(l, cap); e = S - int(np.sum(l)); o = rng.permutation(P); room = (cap - l)[o]; before = np.add.accumulate(room) - room
    l[o] += np.clip(e - before, 0, room); return l
def lens(rng, cap, g):
    c = np.sort(rng.permutation(S - 1)[:P - 1]) + 1
    return fill(rng, np.diff(np.concatenate([[0], c, [S]])), cap)
def put(d, v, g, a, l):
    j = v % V * P; d["frm"][v // V, g, j:j + P] = a; d["ln"][v // V, g, j:j + P] = l
def make(rng, lengths, share):
    d = {"frm": np.zeros((N, 8, V * P), np.int32), "ln": np.zeros((N, 8, V * P), np.int32), "lit": rng.integers(0, 256, (N, 8, Q)).astype(np.int32)}
    for v in range(N * V):
        for g in range(8):
            s = 1.0 if v == 0 else share[v, g]
            l = lengths(rng, Q if s == 1 else S, g); new = (rng.random(P) < s) & (l <= Q)
            put(d, v, g, np.where(new, S + rng.integers(0, np.maximum(Q - l, 0) + 1), rng.integers(0, S - l + 1)), l)
    return d
def setup_inputs(rng):
    return make(rng, lens, np.full((N * V, 8), 0.25))
def setup_inputs_long(rng):
    def lengths(rng, cap, g):
        l = fill(rng, np.ones(P, np.int64), cap)
        return np.sort(l)[::-1].copy() if g == 0 else np.sort(l) if g == 7 else l
    return make(rng, lengths, np.full((N * V, 8), 0.25))
def setup_inputs_ends(rng):
    d = make(rng, lambda rng, cap, g: np.full(P, S // P), np.full((N * V, 8), 0.25))
    k = rng.integers(0, 3, d["frm"].shape); new = d["frm"] >= S
    d["frm"] = np.where(k == 0, np.where(new, S, 0), np.where(k == 1, np.where(new, S + Q, S) - d["ln"], d["frm"])).astype(np.int32)
    return d
def setup_inputs_moves(rng):
    d = setup_inputs(rng)
    for v in range(1, N * V):
        for g in range(8):
            l = lens(rng, S, g); c = np.add.accumulate(l) - l; p = np.arange(P) if g == v % 8 else rng.permutation(P)
            put(d, v, g, c[p], l[p])
    return d
def setup_inputs_spread(rng):
    share = rng.choice(np.array([0, 0.125, 0.5, 1]), (N * V, 8)); share[N * V - 1, 0] = 0; share[N * V - 1, 1] = 1
    d = make(rng, lambda rng, cap, g: fill(rng, 1 + rng.multinomial(S - P, rng.dirichlet(np.full(P, 0.125))), cap), share)
    d["lit"] = np.where(rng.random(d["lit"].shape) < 0.5, 255 * rng.integers(0, 2, d["lit"].shape), d["lit"]).astype(np.int32)
    return d
def check_inputs(d):
    bad = []; a = np.asarray(d["frm"]).astype(np.int64).reshape(N, 8, V, P); l = np.asarray(d["ln"]).astype(np.int64).reshape(N, 8, V, P); t = np.asarray(d["lit"])
    if (l < 1).any() or (np.sum(l, axis=3) != S).any(): bad.append("lengths")
    copied = (a >= 0) & (a + l <= S); new = (a >= S) & (a + l <= S + Q)
    if not (copied | new).all(): bad.append("pieces")
    if not new[0, :, 0].all(): bad.append("version 0")
    if (t < 0).any() or (t > 255).any(): bad.append("literals")
    return bad
def reference(frm, ln, lit):
    y = np.zeros((N, 8, V * S), np.float32); old = np.zeros((8, S), np.int64)
    for v in range(N * V):
        r, k = v // V, v % V; src = np.concatenate([old, lit[r]], axis=1); new = np.zeros((8, S), np.int64)
        for g in range(8):
            a = frm[r, g, k * P:(k + 1) * P]; l = ln[r, g, k * P:(k + 1) * P]; first = np.add.accumulate(l) - l
            new[g] = src[g][np.repeat(a - first, l) + np.arange(S)]
        y[r, :, k * S:(k + 1) * S] = new; old = new
    return {"y": y}

@@ -1,0 +1,262 @@
+from concourse.bass import DstId, RemoteDMATransfer
+from concourse.mybir import AluOpType as A, ActivationFunctionType as F
+
+
+def _bufs():
+    b = {}
+    for dtype, names in (("int32", "X 64 128, CI 64 128, PC 128 4, PCa 128 4"),
+                         ("uint16", "L 128 192, L0r 128 192, L9r 128 64, MU 128 64, M35 128 64, M69 128 64"),
+                         ("float16", "X16 64 136, F16 64 136, C16 64 128, Z 128 144, I128 128 128, PLC 128 64, RS 64 96, "
+                                     "BL 64 256, Sel 64 384, AB 128 1152, E 128 1728, H16 128 1024"),
+                         ("float32", "EI 128 72, K24 64 24, KBL 64 128, KSel 64 128, QR 128 64, QC 128 4, Q0 128 4, KZ 128 144, "
+                                     "ID 128 1280, MP 128 1280, MQ 128 1280, MR 128 1280, V0 128 1280, V1 128 1280, "
+                                     "V2 128 1280, V5 128 1536, Ya 128 1280, Yb 128 1280, Yc 128 1024")):
+        for s in names.split(","):
+            n, p, c = s.split()
+            b[n] = ("sbuf", [int(p), int(c)], dtype)
+    for i in range(8):
+        b["b%d" % i] = ("psum", [128, 512], "float32")
+    return b
+
+
+SCRATCH = _bufs()
+SEMAPHORES = ["sV", "sS", "sP", "sG", "ld", "st", "cp", "lo", "rl0", "rl1", "rl2", "rA", "rB", "rM1", "rM2", "rL9"]
+
+
+def rank_program(g, core, T, topo):
+    r = T.rank_of(core)
+    if r is None:
+        return
+    q = {"V": g.vector, "S": g.scalar, "P": g.tensor, "G": g, "Y": g.sync}
+    cnt = {"V": 0, "S": 0, "P": 0, "G": 0, "lo": 0, "st": 0}
+    seen = {e: {} for e in q}
+
+    def wait(e, deps):
+        for s, n in deps:
+            if seen[e].get(s, 0) < n:
+                q[e].wait_ge(T.sem[s], n)
+                seen[e][s] = n
+
+    def done(e, ins):
+        cnt[e] += 1
+        ins.then_inc(T.sem["s" + e], 1)
+        return ("s" + e, cnt[e])
+
+    def iota(out, pattern, base, cm):
+        return done("G", g.iota(out, pattern, base, cm, allow_small_or_imprecise_dtypes=True))
+
+    def vcopy(out, in_, *deps):
+        wait("V", deps)
+        return done("V", g.vector.tensor_copy(out, in_))
+
+    def ts(out, in0, s1, s2, op0, op1, *deps):
+        wait("V", deps)
+        if op1 is None:
+            return done("V", g.vector.tensor_scalar(out, in0, s1, None, op0))
+        return done("V", g.vector.tensor_scalar(out, in0, s1, s2, op0, op1))
+
+    def tt(out, a, b, op, *deps):
+        wait("V", deps)
+        return done("V", g.vector.tensor_tensor(out, a, b, op))
+
+    def act(out, in_, *deps, bias=0.0):
+        wait("S", deps)
+        if bias:
+            return done("S", g.scalar.activation(out, in_, F.Identity, bias=bias))
+        return done("S", g.scalar.activation(out, in_, F.Copy))
+
+    def mm(out, lhsT, rhs, start, stop, *deps):
+        wait("P", deps)
+        return done("P", g.tensor.matmul(out, lhsT, rhs, start, stop))
+
+    def send(dsts, src, dst, c0, c1, sem, few, *deps):
+        wait("G", deps)
+        cores = [T.cores[d] for d in dsts]
+        eng = topo.engines(core, cores[0])
+        if few:
+            eng = eng[::2]
+        at = [topo.addr(c) for c in cores]
+        g.remote_dma_fused([RemoteDMATransfer(dst_ids=[DstId(rid=a[0], pnc=a[1]) for a in at],
+                                              dma_engine_mask=sum(1 << e for e in eng), remote_sem=T.sem[sem],
+                                              srcs=[T[src][:, c0:c1]], dsts=[T[dst][:, c0:c1] for c in cores])],
+                           local_sem=T.sem.lo)
+        cnt["lo"] += len(eng)
+
+    def arrived(sem, few=False):
+        eng = topo.engines(T.cores[0] if r else T.cores[1], core)
+        return (sem, len(eng[::2] if few else eng))
+
+    def gather(out, win, lst, c0, deps, kv=32):
+        wait("V", deps)
+        a = done("V", g.vector.tensor_copy(T[out][:, 0:16 * kv], win.indirect(T[lst][:, c0:c0 + kv])))
+        wait("S", deps)
+        b = done("S", g.scalar.activation(T[out][:, 16 * kv:1024], win.indirect(T[lst][:, c0 + kv:c0 + 64]), F.Copy))
+        return [a, b]
+
+    g.sync.dma_start(T.X[32:56, :], T.ln[:]).then_inc(T.sem.ld, 16)
+    g.scalar.dma_start(T.X[0:24, :], T.frm[:]).then_inc(T.sem.ld, 16)
+    g.sync.dma_start(T.X[24:32, :], T.lit[:, 0:128]).then_inc(T.sem.ld, 16)
+    g.scalar.dma_start(T.X[56:64, :], T.lit[:, 128:256]).then_inc(T.sem.ld, 16)
+
+    dEI = iota(T.EI[:, 0:65], [[16, 65]], 0, 0)
+    d24 = iota(T.K24[:, :], [[-1, 3], [-3, 8]], 0, 1)
+    dBL = iota(T.KBL[:, :], [[-1, 8], [0, 16]], -24, 1)
+    dSel = iota(T.KSel[:, :], [[-3, 2], [0, 16], [-6, 4]], -32, 1)
+    dPC = done("G", g.iota(T.PC[:, 0:1], [[0, 1]], 0, 1))
+    dKZ = iota(T.KZ[:, 0:143], [[1, 143]], -15, -1)
+    dQR = iota(T.QR[:, :], [[1, 16], [0, 4]], 0, 0)
+    compose = r in (1, 2)
+    if compose:
+        dID0 = iota(T.ID[:, 0:640], [[1, 640]], 0, 0)
+    vcopy(T.X16[:, 0:1], T.EI[0:64, 0:1], dEI)
+    vcopy(T.F16[:, 0:1], T.EI[0:64, 0:1])
+    for j in range(6):
+        ts(T.AB[:, 192 * j + 64:192 * j + 128], T.EI[:, 0:64], 0.0, None, A.mult, None)
+    ts(T.RS[:, 0:24], T.K24[:, :], 0.0, None, A.is_equal, None, d24)
+    ts(T.RS[:, 24:48], T.K24[:, :], 0.0, -1.0, A.is_equal, A.mult)
+    ts(T.RS[:, 48:72], T.K24[:, :], 32.0, -1.0, A.is_equal, A.mult)
+    dRS = ts(T.RS[:, 72:96], T.K24[:, :], 32.0, None, A.is_equal, None)
+    ts(T.BL[:, 0:128], T.KBL[:, :], 0.0, None, A.is_equal, None, dBL)
+    dBLc = ts(T.BL[:, 128:256], T.KBL[:, :], 32.0, None, A.is_equal, None)
+    for k in range(3):
+        dSelc = ts(T.Sel[:, 128 * k:128 * k + 128], T.KSel[:, :], float(k), None, A.is_equal, None, dSel)
+    d = ts(T.PCa[:, 0:1], T.PC[:, 0:1], 15, None, A.bitwise_and, None, dPC)
+    dI = ts(T.I128[:, :], T.KZ[:, 15:143], 0.0, None, A.is_equal, None, dKZ)
+    d = vcopy(T.QC[:, 0:1], T.PCa[:, 0:1], d)
+
+    dX = vcopy(T.X16[:, 1:129], T.X[:, :], ("ld", 64))
+    wait("V", [dX])
+    dF = done("V", g.vector.tensor_tensor_scan(T.F16[32:56, 1:129], T.X16[32:56, 1:129], T.X16[32:56, 1:129], 0.0, A.add, A.max))
+    dC = ts(T.CI[32:56, :], T.F16[32:56, 0:128], 0.0625, -0.46875, A.mult, A.add, dF)
+    dC = ts(T.C16[32:56, :], T.CI[32:56, :], -16.0, None, A.mult, None, dC)
+    dPL = ts(T.PLC[:, :], T.EI[:, 0:64], T.QC[:, 0:1], None, A.add, None, d)
+
+    mm(T.b0[:, 32:56], T.X16[:, 1:129], T.RS[:, 0:24], True, False, dRS, dX)
+    mm(T.b0[:, 32:56], T.X16[:, 0:128], T.RS[:, 24:48], False, False)
+    mm(T.b0[:, 32:56], T.X16[:, 0:128], T.RS[:, 48:72], False, True)
+    dFT = mm(T.b0[:, 0:24], T.F16[32:56, 0:128], T.RS[32:56, 72:96], True, True, dF)
+    qb = [T.b2, T.b3, T.b4]
+    lb = [T.b5, T.b6, T.b7]
+    for k in range(3):
+        mm(qb[k][:, 0:128], T.F16[32:56, 0:128], T.Sel[32:56, 128 * k:128 * k + 128], True, False, dSelc)
+    mm(T.b1[:, 0:128], T.BL[:, 0:128], T.X16[:, 1:129], True, True, dBLc)
+    dLR = mm(T.b1[:, 128:256], T.BL[:, 128:256], T.X16[:, 1:129], True, True)
+    dQ = []
+    for k in range(3):
+        dQ.append(mm(qb[k][:, 0:128], T.C16[32:56, :], T.Sel[32:56, 128 * k:128 * k + 128], False, True, dC))
+
+    tails = [[("V0", 1024), ("V1", 1024)], [("V2", 1024), ("Ya", 1024), ("Yb", 1024)],
+             [("V5", 1024), ("Ya", 1024), ("Yb", 1024)], [("V5", 1280), ("Ya", 1024), ("Yb", 1024)]][r]
+    dT = {}
+    for b, c in tails:
+        dT[b] = act(T[b][:, c:c + 256], T.b1[:, 0:256], dLR)
+    if r < 3:
+        b = tails[0][0]
+        send([[1, 2, 3], [2, 3], [3]][r], b, b, 1024, 1280, "rl%d" % r, False, dT[b])
+    if compose:
+        dID = act(T.ID[:, 640:1280], T.ID[:, 0:640], dID0, bias=640.0)
+        dMP = act(T.MP[:, 1024:1280], T.ID[:, 1024:1280], dID)
+        dMQ = act(T.MQ[:, 1024:1280], T.ID[:, 1024:1280])
+        if r == 2:
+            dMR = act(T.MR[:, 1024:1280], T.ID[:, 1024:1280], bias=256.0)
+
+    def e_op(k, gd):
+        s = 8 * k + gd
+        e0 = 576 * k + 72 * gd
+        return ts(T.E[:, e0:e0 + 65], T.EI[:, 0:65], T.b0[:, s:s + 1], T.b0[:, 32 + s:33 + s], A.is_gt, A.mult, dFT)
+
+    def steps(k):
+        dE = [e_op(k, gd) for gd in range(4)]
+        o = 384 * k
+        tt(T.AB[:, o:o + 64], qb[k][:, 0:64], T.QR[:, :], A.is_le, dQ[k], dQR)
+        tt(T.AB[:, o + 192:o + 256], qb[k][:, 0:64], T.QR[:, :], A.is_gt)
+        tt(T.AB[:, o + 128:o + 192], qb[k][:, 64:128], T.QR[:, :], A.is_le)
+        dA = tt(T.AB[:, o + 320:o + 384], qb[k][:, 64:128], T.QR[:, :], A.is_gt)
+        dE += [e_op(k, gd) for gd in range(4, 8)]
+        mm(lb[k][:, 0:64], T.I128[:, :], T.PLC[:, :], True, False, dI, dPL)
+        for gd in range(8):
+            a, par = gd // 2, gd % 2
+            e0 = 576 * k + 72 * gd
+            out = lb[k][32 * a:32 * a + 32, 0:64]
+            s0 = o + 64 * par + a
+            mm(out, T.AB[:, s0:s0 + 125:4], T.E[:, e0 + 1:e0 + 65], False, False, dA, dE[gd])
+            dl = mm(out, T.AB[:, s0 + 192:s0 + 317:4], T.E[:, e0:e0 + 64], False, par == 1)
+        return dl
+
+    def take(k, dl):
+        out = T.L[:, 64 * k:64 * k + 64]
+        if r == 0 and k == 0:
+            return ts(out, lb[k][:, 0:64], -1024.0, None, A.add, None, dl)
+        return vcopy(out, lb[k][:, 0:64], dl)
+
+    dl0 = steps(0)
+    dl1 = steps(1)
+    dL = [take(0, dl0)]
+    if r == 3:
+        send([2], "L", "L9r", 0, 64, "rL9", True, dL[0])
+    dl2 = steps(2)
+
+    def store(k, b, deps):
+        wait("Y", deps)
+        g.sync.dma_start(T.y[:, 1024 * k:1024 * k + 1024], T[b][0:128:16, 0:1024]).then_inc(T.sem.st, 16)
+        cnt["st"] += 16
+
+    def store_last(deps):
+        wait("Y", deps[:1])
+        g.sync.dma_start(T.y[:, 2048:2560], T.Yc[0:128:16, 0:512]).then_inc(T.sem.st, 16)
+        wait("S", deps[1:])
+        g.scalar.dma_start(T.y[:, 2560:3072], T.Yc[0:128:16, 512:1024]).then_inc(T.sem.st, 16)
+        cnt["st"] += 32
+
+    if r == 0:
+        d = gather("V0", T.V0[:, 1024:1280], "L", 0, [dL[0], dT["V0"]], 20)
+        dL.append(take(1, dl1))
+        send([1, 2, 3], "L", "L0r", 0, 128, "rA", False, dL[1])
+        store(0, "V0", d)
+        d = gather("V1", T.V0[:, 0:1280], "L", 64, d + [dL[1]])
+        dL.append(take(2, dl2))
+        send([1, 2, 3], "L", "L0r", 128, 192, "rB", False, dL[2])
+        store(1, "V1", d)
+        store_last(gather("Yc", T.V1[:, 0:1280], "L", 128, d + [dL[2], dT["V1"]]))
+    else:
+        if compose:
+            d = gather("MP", T.ID[:, 0:1280], "L", 0, [dL[0], dID], 20)
+        dL.append(take(1, dl1))
+        if compose:
+            dZ = ts(T.Q0[:, 0:1], T.QC[:, 0:1], 0.0, None, A.is_equal, None)
+            dZ = ts(T.Z[:, 0:143], T.KZ[:, 0:143], 0.0, T.Q0[:, 0:1], A.is_equal, A.mult, dZ)
+            d = gather("MQ", T.MP[:, 0:1280], "L", 64, d + [dL[1], dMP])
+        dL.append(take(2, dl2))
+        if compose:
+            if r == 1:
+                d = gather("H16", T.MQ[:, 0:1280], "L", 128, d + [dL[2], dMQ])
+            else:
+                d = gather("MR", T.MQ[:, 0:1280], "L", 128, d + [dL[2], dMQ])
+                d = gather("H16", T.MR[:, 0:1280], "L9r", 0, d + [dMR, arrived("rL9", True)])
+            for t in range(16):
+                dc = mm(T.b2[:, 0:64], T.Z[:, 15 - t:143 - t], T.H16[:, t:1024:16], t == 0, t == 15, dZ, *d)
+            dM = vcopy(T.MU[:, :], T.b2[:, 0:64], dc)
+            if r == 1:
+                send([2, 3], "MU", "M35", 0, 64, "rM1", False, dM)
+            else:
+                send([3], "MU", "M69", 0, 64, "rM2", False, dM)
+        rl0 = arrived("rl0")
+        wait("Y", [rl0])
+        g.sync.dma_start(T.V1[:, 1024:1280], T.V0[:, 1024:1280]).then_inc(T.sem.cp, 16)
+        d = gather("V0", T.V0[:, 1024:1280], "L0r", 0, [rl0, arrived("rA")])
+        d = gather("V1", T.V0[:, 0:1280], "L0r", 64, d)
+        d = gather("V2", T.V1[:, 0:1280], "L0r", 128, d + [arrived("rB"), ("cp", 16)])
+        if r == 1:
+            d = gather("Ya", T.V2[:, 0:1280], "L", 0, d + [dT["V2"], dL[0]])
+        else:
+            d = gather("V5", T.V2[:, 0:1280], "M35", 0, d + [arrived("rl1"), arrived("rM1")])
+            if r == 2:
+                d = gather("Ya", T.V5[:, 0:1280], "L", 0, d + [dT["V5"], dL[0]])
+            else:
+                d = gather("Ya", T.V5[:, 0:1536], "M69", 0, d + [dT["V5"], arrived("rl2"), arrived("rM2")])
+        store(0, "Ya", d)
+        d = gather("Yb", T.Ya[:, 0:1280], "L", 64, d + [dT["Ya"], dL[1]])
+        store(1, "Yb", d)
+        store_last(gather("Yc", T.Yb[:, 0:1280], "L", 128, d + [dT["Yb"], dL[2]]))
+    wait("Y", [("st", cnt["st"])])
+    wait("G", [("sV", cnt["V"]), ("sS", cnt["S"]), ("sP", cnt["P"]), ("sG", cnt["G"]), ("lo", cnt["lo"])])

@@ -8,9 +8,10 @@ def _bufs():
                          ("uint16", "L 128 192, L0r 128 192, L9r 128 64, MU 128 64, M35 128 64, M69 128 64"),
                          ("float16", "X16 64 136, F16 64 136, C16 64 128, Z 128 144, I128 128 128, PLC 128 64, RS 64 96, "
                                      "BL 64 256, Sel 64 384, AB 128 1152, E 128 1728, H16 128 1024"),
+                         ("bfloat16", "V0 128 1280, V1 128 1280, V2 128 1280, V5 128 1536"),
                          ("float32", "EI 128 72, K24 64 24, KBL 64 128, KSel 64 128, QR 128 64, QC 128 4, Q0 128 4, KZ 128 144, "
-                                     "ID 128 1280, MP 128 1280, MQ 128 1280, MR 128 1280, V0 128 1280, V1 128 1280, "
-                                     "V2 128 1280, V5 128 1536, Ya 128 1280, Yb 128 1280, Yc 128 1024")):
+                                     "AZ 128 128, AS 64 256, ID 128 1280, MP 128 1280, MQ 128 1280, MR 128 1280, "
+                                     "Ya 128 1280, Yb 128 1280, Yc 128 1024")):
         for s in names.split(","):
             n, p, c = s.split()
             b[n] = ("sbuf", [int(p), int(c)], dtype)
@@ -20,7 +21,7 @@ def _bufs():
 
 
 SCRATCH = _bufs()
-SEMAPHORES = ["sV", "sS", "sP", "sG", "ld", "st", "cp", "lo", "rl0", "rl1", "rl2", "rA", "rB", "rM1", "rM2", "rL9"]
+SEMAPHORES = ["sV", "sS", "sP", "sG", "ld", "st", "sc", "lo", "rl0", "rl1", "rl2", "rA0", "rA1", "rA2", "rV", "rM1", "rM2", "rL9"]
 
 
 def rank_program(g, core, T, topo):
@@ -59,11 +60,9 @@ def rank_program(g, core, T, topo):
         wait("V", deps)
         return done("V", g.vector.tensor_tensor(out, a, b, op))
 
-    def act(out, in_, *deps, bias=0.0):
+    def act(out, in_, *deps, func=F.Identity, bias=0.0, scale=1.0):
         wait("S", deps)
-        if bias:
-            return done("S", g.scalar.activation(out, in_, F.Identity, bias=bias))
-        return done("S", g.scalar.activation(out, in_, F.Copy))
+        return done("S", g.scalar.activation(out, in_, func, bias=bias, scale=scale))
 
     def mm(out, lhsT, rhs, start, stop, *deps):
         wait("P", deps)
@@ -93,146 +92,178 @@ def rank_program(g, core, T, topo):
         b = done("S", g.scalar.activation(T[out][:, 16 * kv:1024], win.indirect(T[lst][:, c0 + kv:c0 + 64]), F.Copy))
         return [a, b]
 
+    compose = r in (1, 2)
     g.sync.dma_start(T.X[32:56, :], T.ln[:]).then_inc(T.sem.ld, 16)
     g.scalar.dma_start(T.X[0:24, :], T.frm[:]).then_inc(T.sem.ld, 16)
     g.sync.dma_start(T.X[24:32, :], T.lit[:, 0:128]).then_inc(T.sem.ld, 16)
     g.scalar.dma_start(T.X[56:64, :], T.lit[:, 128:256]).then_inc(T.sem.ld, 16)
 
+    def iota_bl():
+        return iota(T.KBL[:, :], [[-1, 8], [0, 16]], -24, 1)
+
     dEI = iota(T.EI[:, 0:65], [[16, 65]], 0, 0)
     d24 = iota(T.K24[:, :], [[-1, 3], [-3, 8]], 0, 1)
-    dBL = iota(T.KBL[:, :], [[-1, 8], [0, 16]], -24, 1)
+    if r == 0:
+        dBL = iota_bl()
     dSel = iota(T.KSel[:, :], [[-3, 2], [0, 16], [-6, 4]], -32, 1)
     dPC = done("G", g.iota(T.PC[:, 0:1], [[0, 1]], 0, 1))
     dKZ = iota(T.KZ[:, 0:143], [[1, 143]], -15, -1)
     dQR = iota(T.QR[:, :], [[1, 16], [0, 4]], 0, 0)
-    compose = r in (1, 2)
     if compose:
         dID0 = iota(T.ID[:, 0:640], [[1, 640]], 0, 0)
+    if r:
+        dBL = iota_bl()
+    for j in range(6):
+        dZero = act(T.AB[:, 192 * j + 64:192 * j + 128], T.EI[:, 0:64], dEI, scale=0.0)
+    d1 = act(T.AS[:, 0:128], T.KSel[:, :], dSel, func=F.Abs, bias=-1.0)
+    d2 = act(T.AS[:, 128:256], T.KSel[:, :], func=F.Abs, bias=-2.0)
+    d3 = act(T.AZ[:, :], T.KZ[:, 15:143], dKZ, func=F.Abs)
+    act(T.Sel[:, 128:256], T.AS[:, 0:128], d1, func=F.Relu, bias=1.0, scale=-1.0)
+    dSelS = act(T.Sel[:, 256:384], T.AS[:, 128:256], d2, func=F.Relu, bias=1.0, scale=-1.0)
+    dI = act(T.I128[:, :], T.AZ[:, :], d3, func=F.Relu, bias=1.0, scale=-1.0)
+
+    def one_hot_bl():
+        ts(T.BL[:, 0:128], T.KBL[:, :], 0.0, None, A.is_equal, None, dBL)
+        return ts(T.BL[:, 128:256], T.KBL[:, :], 32.0, None, A.is_equal, None)
+
     vcopy(T.X16[:, 0:1], T.EI[0:64, 0:1], dEI)
     vcopy(T.F16[:, 0:1], T.EI[0:64, 0:1])
-    for j in range(6):
-        ts(T.AB[:, 192 * j + 64:192 * j + 128], T.EI[:, 0:64], 0.0, None, A.mult, None)
     ts(T.RS[:, 0:24], T.K24[:, :], 0.0, None, A.is_equal, None, d24)
     ts(T.RS[:, 24:48], T.K24[:, :], 0.0, -1.0, A.is_equal, A.mult)
     ts(T.RS[:, 48:72], T.K24[:, :], 32.0, -1.0, A.is_equal, A.mult)
     dRS = ts(T.RS[:, 72:96], T.K24[:, :], 32.0, None, A.is_equal, None)
-    ts(T.BL[:, 0:128], T.KBL[:, :], 0.0, None, A.is_equal, None, dBL)
-    dBLc = ts(T.BL[:, 128:256], T.KBL[:, :], 32.0, None, A.is_equal, None)
-    for k in range(3):
-        dSelc = ts(T.Sel[:, 128 * k:128 * k + 128], T.KSel[:, :], float(k), None, A.is_equal, None, dSel)
+    if r == 0:
+        dBLc = one_hot_bl()
+    dSel0 = ts(T.Sel[:, 0:128], T.KSel[:, :], 0.0, None, A.is_equal, None, dSel)
     d = ts(T.PCa[:, 0:1], T.PC[:, 0:1], 15, None, A.bitwise_and, None, dPC)
-    dI = ts(T.I128[:, :], T.KZ[:, 15:143], 0.0, None, A.is_equal, None, dKZ)
     d = vcopy(T.QC[:, 0:1], T.PCa[:, 0:1], d)
+    dPL = ts(T.PLC[:, :], T.EI[:, 0:64], T.QC[:, 0:1], None, A.add, None, d)
+    if compose:
+        d = ts(T.Q0[:, 0:1], T.QC[:, 0:1], 0.0, None, A.is_equal, None)
+        dZ = ts(T.Z[:, 0:143], T.KZ[:, 0:143], 0.0, T.Q0[:, 0:1], A.is_equal, A.mult, d, dKZ)
 
     dX = vcopy(T.X16[:, 1:129], T.X[:, :], ("ld", 64))
     wait("V", [dX])
     dF = done("V", g.vector.tensor_tensor_scan(T.F16[32:56, 1:129], T.X16[32:56, 1:129], T.X16[32:56, 1:129], 0.0, A.add, A.max))
     dC = ts(T.CI[32:56, :], T.F16[32:56, 0:128], 0.0625, -0.46875, A.mult, A.add, dF)
     dC = ts(T.C16[32:56, :], T.CI[32:56, :], -16.0, None, A.mult, None, dC)
-    dPL = ts(T.PLC[:, :], T.EI[:, 0:64], T.QC[:, 0:1], None, A.add, None, d)
+
+    def literals():
+        mm(T.b1[:, 0:128], T.BL[:, 0:128], T.X16[:, 1:129], True, True, dBLc)
+        return mm(T.b1[:, 128:256], T.BL[:, 128:256], T.X16[:, 1:129], True, True)
+
+    qb = [T.b2, T.b3, T.b4]
+    lb = [T.b5, T.b6, T.b7]
+
+    def remainders(k, *deps):
+        sel = T.Sel[32:56, 128 * k:128 * k + 128]
+        mm(qb[k][:, 0:128], T.F16[32:56, 0:128], sel, True, False, *deps)
+        return mm(qb[k][:, 0:128], T.C16[32:56, :], sel, False, True, dC)
 
     mm(T.b0[:, 32:56], T.X16[:, 1:129], T.RS[:, 0:24], True, False, dRS, dX)
     mm(T.b0[:, 32:56], T.X16[:, 0:128], T.RS[:, 24:48], False, False)
     mm(T.b0[:, 32:56], T.X16[:, 0:128], T.RS[:, 48:72], False, True)
+    if r == 0:
+        dLR = literals()
     dFT = mm(T.b0[:, 0:24], T.F16[32:56, 0:128], T.RS[32:56, 72:96], True, True, dF)
-    qb = [T.b2, T.b3, T.b4]
-    lb = [T.b5, T.b6, T.b7]
-    for k in range(3):
-        mm(qb[k][:, 0:128], T.F16[32:56, 0:128], T.Sel[32:56, 128 * k:128 * k + 128], True, False, dSelc)
-    mm(T.b1[:, 0:128], T.BL[:, 0:128], T.X16[:, 1:129], True, True, dBLc)
-    dLR = mm(T.b1[:, 128:256], T.BL[:, 128:256], T.X16[:, 1:129], True, True)
-    dQ = []
-    for k in range(3):
-        dQ.append(mm(qb[k][:, 0:128], T.C16[32:56, :], T.Sel[32:56, 128 * k:128 * k + 128], False, True, dC))
+    dQ = [remainders(0, dSel0), remainders(1, dSelS)]
 
-    tails = [[("V0", 1024), ("V1", 1024)], [("V2", 1024), ("Ya", 1024), ("Yb", 1024)],
-             [("V5", 1024), ("Ya", 1024), ("Yb", 1024)], [("V5", 1280), ("Ya", 1024), ("Yb", 1024)]][r]
+    tails = [("V0", 1024), ("V2", 1024), ("V5", 1024), ("V5", 1280)][r:r + 1] + [("Ya", 1024), ("Yb", 1024)]
     dT = {}
-    for b, c in tails:
+
+    def tail(i):
+        b, c = tails[i]
         dT[b] = act(T[b][:, c:c + 256], T.b1[:, 0:256], dLR)
-    if r < 3:
-        b = tails[0][0]
-        send([[1, 2, 3], [2, 3], [3]][r], b, b, 1024, 1280, "rl%d" % r, False, dT[b])
+        if i == 0 and r < 3:
+            send([[1, 3], [2, 3], [3]][r], b, b, c, c + 256, "rl%d" % r, False, dT[b])
+
+    if r == 0:
+        for i in range(3):
+            tail(i)
     if compose:
         dID = act(T.ID[:, 640:1280], T.ID[:, 0:640], dID0, bias=640.0)
-        dMP = act(T.MP[:, 1024:1280], T.ID[:, 1024:1280], dID)
-        dMQ = act(T.MQ[:, 1024:1280], T.ID[:, 1024:1280])
+        dMP = iota(T.MP[:, 1024:1280], [[1, 256]], 1024, 0)
+        dMQ = iota(T.MQ[:, 1024:1280], [[1, 256]], 1024, 0)
         if r == 2:
-            dMR = act(T.MR[:, 1024:1280], T.ID[:, 1024:1280], bias=256.0)
+            dMR = iota(T.MR[:, 1024:1280], [[1, 256]], 1280, 0)
 
     def e_op(k, gd):
         s = 8 * k + gd
         e0 = 576 * k + 72 * gd
         return ts(T.E[:, e0:e0 + 65], T.EI[:, 0:65], T.b0[:, s:s + 1], T.b0[:, 32 + s:33 + s], A.is_gt, A.mult, dFT)
 
-    def steps(k):
+    def steps_v(k):
         dE = [e_op(k, gd) for gd in range(4)]
         o = 384 * k
         tt(T.AB[:, o:o + 64], qb[k][:, 0:64], T.QR[:, :], A.is_le, dQ[k], dQR)
         tt(T.AB[:, o + 192:o + 256], qb[k][:, 0:64], T.QR[:, :], A.is_gt)
         tt(T.AB[:, o + 128:o + 192], qb[k][:, 64:128], T.QR[:, :], A.is_le)
         dA = tt(T.AB[:, o + 320:o + 384], qb[k][:, 64:128], T.QR[:, :], A.is_gt)
-        dE += [e_op(k, gd) for gd in range(4, 8)]
+        return dA, dE + [e_op(k, gd) for gd in range(4, 8)]
+
+    def steps_p(k, dA, dE):
+        o = 384 * k
         mm(lb[k][:, 0:64], T.I128[:, :], T.PLC[:, :], True, False, dI, dPL)
         for gd in range(8):
             a, par = gd // 2, gd % 2
             e0 = 576 * k + 72 * gd
             out = lb[k][32 * a:32 * a + 32, 0:64]
             s0 = o + 64 * par + a
-            mm(out, T.AB[:, s0:s0 + 125:4], T.E[:, e0 + 1:e0 + 65], False, False, dA, dE[gd])
+            mm(out, T.AB[:, s0:s0 + 125:4], T.E[:, e0 + 1:e0 + 65], False, False, dZero, dA, dE[gd])
             dl = mm(out, T.AB[:, s0 + 192:s0 + 317:4], T.E[:, e0:e0 + 64], False, par == 1)
         return dl
 
     def take(k, dl):
         out = T.L[:, 64 * k:64 * k + 64]
         if r == 0 and k == 0:
-            return ts(out, lb[k][:, 0:64], -1024.0, None, A.add, None, dl)
-        return vcopy(out, lb[k][:, 0:64], dl)
+            dL.append(ts(out, lb[k][:, 0:64], -1024.0, None, A.add, None, dl))
+        else:
+            dL.append(vcopy(out, lb[k][:, 0:64], dl))
+        if r == 0:
+            send([1, 3], "L", "L0r", 64 * k, 64 * k + 64, "rA%d" % k, False, dL[k])
+        if r == 3 and k == 0:
+            send([2], "L", "L9r", 0, 64, "rL9", True, dL[0])
 
-    dl0 = steps(0)
-    dl1 = steps(1)
-    dL = [take(0, dl0)]
-    if r == 3:
-        send([2], "L", "L9r", 0, 64, "rL9", True, dL[0])
-    dl2 = steps(2)
+    dL = []
+    dl0 = steps_p(0, *steps_v(0))
+    dQ.append(remainders(2))
+    dl1 = steps_p(1, *steps_v(1))
+    take(0, dl0)
+    if r:
+        dBLc = one_hot_bl()
+        dLR = literals()
+    dl2 = steps_p(2, *steps_v(2))
 
     def store(k, b, deps):
         wait("Y", deps)
         g.sync.dma_start(T.y[:, 1024 * k:1024 * k + 1024], T[b][0:128:16, 0:1024]).then_inc(T.sem.st, 16)
         cnt["st"] += 16
 
-    def store_last(deps):
-        wait("Y", deps[:1])
-        g.sync.dma_start(T.y[:, 2048:2560], T.Yc[0:128:16, 0:512]).then_inc(T.sem.st, 16)
-        wait("S", deps[1:])
-        g.scalar.dma_start(T.y[:, 2560:3072], T.Yc[0:128:16, 512:1024]).then_inc(T.sem.st, 16)
-        cnt["st"] += 32
-
     if r == 0:
-        d = gather("V0", T.V0[:, 1024:1280], "L", 0, [dL[0], dT["V0"]], 20)
-        dL.append(take(1, dl1))
-        send([1, 2, 3], "L", "L0r", 0, 128, "rA", False, dL[1])
-        store(0, "V0", d)
-        d = gather("V1", T.V0[:, 0:1280], "L", 64, d + [dL[1]])
-        dL.append(take(2, dl2))
-        send([1, 2, 3], "L", "L0r", 128, 192, "rB", False, dL[2])
-        store(1, "V1", d)
-        store_last(gather("Yc", T.V1[:, 0:1280], "L", 128, d + [dL[2], dT["V1"]]))
+        d = gather("Ya", T.V0[:, 1024:1280], "L", 0, [dL[0], dT["V0"]], 18)
+        store(0, "Ya", d)
+        take(1, dl1)
+        d = gather("Yb", T.Ya[:, 0:1280], "L", 64, d + [dL[1], dT["Ya"]])
+        store(1, "Yb", d)
+        take(2, dl2)
+        d = gather("V2", T.Yb[:, 0:1280], "L", 128, d + [dL[2], dT["Yb"]])
+        send([2], "V2", "V2", 0, 1024, "rV", False, *d)
+        g.dma_start(T.y[:, 2048:3072], T.V2[0:128:16, 0:1024]).then_inc(T.sem.sc, 16)
+        wait("G", [("sc", 16)])
     else:
         if compose:
-            d = gather("MP", T.ID[:, 0:1280], "L", 0, [dL[0], dID], 20)
-        dL.append(take(1, dl1))
+            d = gather("MP", T.ID[:, 0:1280], "L", 0, [dL[0], dID], 18)
+        take(1, dl1)
+        tail(0)
         if compose:
-            dZ = ts(T.Q0[:, 0:1], T.QC[:, 0:1], 0.0, None, A.is_equal, None)
-            dZ = ts(T.Z[:, 0:143], T.KZ[:, 0:143], 0.0, T.Q0[:, 0:1], A.is_equal, A.mult, dZ)
             d = gather("MQ", T.MP[:, 0:1280], "L", 64, d + [dL[1], dMP])
-        dL.append(take(2, dl2))
+        take(2, dl2)
+        if r == 1:
+            d = gather("H16", T.MQ[:, 0:1280], "L", 128, d + [dL[2], dMQ])
+        if r == 2:
+            d = gather("MR", T.MQ[:, 0:1280], "L", 128, d + [dL[2], dMQ])
+            d = gather("H16", T.MR[:, 0:1280], "L9r", 0, d + [dMR, arrived("rL9", True)])
         if compose:
-            if r == 1:
-                d = gather("H16", T.MQ[:, 0:1280], "L", 128, d + [dL[2], dMQ])
-            else:
-                d = gather("MR", T.MQ[:, 0:1280], "L", 128, d + [dL[2], dMQ])
-                d = gather("H16", T.MR[:, 0:1280], "L9r", 0, d + [dMR, arrived("rL9", True)])
             for t in range(16):
                 dc = mm(T.b2[:, 0:64], T.Z[:, 15 - t:143 - t], T.H16[:, t:1024:16], t == 0, t == 15, dZ, *d)
             dM = vcopy(T.MU[:, :], T.b2[:, 0:64], dc)
@@ -240,12 +271,15 @@ def rank_program(g, core, T, topo):
                 send([2, 3], "MU", "M35", 0, 64, "rM1", False, dM)
             else:
                 send([3], "MU", "M69", 0, 64, "rM2", False, dM)
-        rl0 = arrived("rl0")
-        wait("Y", [rl0])
-        g.sync.dma_start(T.V1[:, 1024:1280], T.V0[:, 1024:1280]).then_inc(T.sem.cp, 16)
-        d = gather("V0", T.V0[:, 1024:1280], "L0r", 0, [rl0, arrived("rA")])
-        d = gather("V1", T.V0[:, 0:1280], "L0r", 64, d)
-        d = gather("V2", T.V1[:, 0:1280], "L0r", 128, d + [arrived("rB"), ("cp", 16)])
+        tail(1)
+        tail(2)
+        if r == 2:
+            d = [arrived("rV")]
+        else:
+            d = gather("V0", T.V0[:, 1024:1280], "L0r", 0, [arrived("rl0"), arrived("rA0")])
+            dV1 = act(T.V1[:, 1024:1280], T.V0[:, 1024:1280])
+            d = gather("V1", T.V0[:, 0:1280], "L0r", 64, d + [arrived("rA1")], 36)
+            d = gather("V2", T.V1[:, 0:1280], "L0r", 128, d + [arrived("rA2"), dV1])
         if r == 1:
             d = gather("Ya", T.V2[:, 0:1280], "L", 0, d + [dT["V2"], dL[0]])
         else:
@@ -257,6 +291,11 @@ def rank_program(g, core, T, topo):
         store(0, "Ya", d)
         d = gather("Yb", T.Ya[:, 0:1280], "L", 64, d + [dT["Ya"], dL[1]])
         store(1, "Yb", d)
-        store_last(gather("Yc", T.Yb[:, 0:1280], "L", 128, d + [dT["Yb"], dL[2]]))
+        d = gather("Yc", T.Yb[:, 0:1280], "L", 128, d + [dT["Yb"], dL[2]])
+        wait("Y", d[:1])
+        g.sync.dma_start(T.y[:, 2048:2560], T.Yc[0:128:16, 0:512]).then_inc(T.sem.st, 16)
+        wait("S", d[1:])
+        g.scalar.dma_start(T.y[:, 2560:3072], T.Yc[0:128:16, 512:1024]).then_inc(T.sem.st, 16)
+        cnt["st"] += 32
     wait("Y", [("st", cnt["st"])])
     wait("G", [("sV", cnt["V"]), ("sS", cnt["S"]), ("sP", cnt["P"]), ("sG", cnt["G"]), ("lo", cnt["lo"])])

@@ -4,13 +4,13 @@ from concourse.mybir import AluOpType as A, ActivationFunctionType as F
 
 def _bufs():
     b = {}
-    for dtype, names in (("int32", "X 64 128, CI 64 128, PC 128 4, PCa 128 4"),
+    for dtype, names in (("int32", "X 64 128, PC 128 4, PCa 128 4"),
                          ("uint16", "L 128 192, L0r 128 192, L9r 128 64, MU 128 64, M35 128 64, M69 128 64"),
-                         ("float16", "X16 64 136, F16 64 136, C16 64 128, Z 128 144, I128 128 128, PLC 128 64, RS 64 96, "
-                                     "BL 64 256, Sel 64 384, AB 128 1152, E 128 1728, H16 128 1024"),
-                         ("bfloat16", "V0 128 1280, V1 128 1280, V2 128 1280, V5 128 1536"),
-                         ("float32", "EI 128 72, K24 64 24, KBL 64 128, KSel 64 128, QR 128 64, QC 128 4, Q0 128 4, KZ 128 144, "
-                                     "AZ 128 128, AS 64 256, ID 128 1280, MP 128 1280, MQ 128 1280, MR 128 1280, "
+                         ("float16", "X16 64 136, F16 64 136, B16 64 128, Z 128 144, RS 64 96, BL 64 256, Sel 64 384, "
+                                     "Sg 128 384, AB 128 1216, E 128 1728, H16 128 1024"),
+                         ("bfloat16", "EI 128 72, QN 128 128, ONE 128 128, V0 128 1280, V1 128 1280, V2 128 1280, V5 128 1536"),
+                         ("float32", "K24 64 24, KBL 64 128, KSel 64 64, QC 128 4, Q0 128 4, KZ 128 144, "
+                                     "ID 128 1280, MP 128 1280, MQ 128 1280, MR 128 1280, "
                                      "Ya 128 1280, Yb 128 1280, Yc 128 1024")):
         for s in names.split(","):
             n, p, c = s.split()
@@ -56,10 +56,6 @@ def rank_program(g, core, T, topo):
             return done("V", g.vector.tensor_scalar(out, in0, s1, None, op0))
         return done("V", g.vector.tensor_scalar(out, in0, s1, s2, op0, op1))
 
-    def tt(out, a, b, op, *deps):
-        wait("V", deps)
-        return done("V", g.vector.tensor_tensor(out, a, b, op))
-
     def act(out, in_, *deps, func=F.Identity, bias=0.0, scale=1.0):
         wait("S", deps)
         return done("S", g.scalar.activation(out, in_, func, bias=bias, scale=scale))
@@ -85,11 +81,11 @@ def rank_program(g, core, T, topo):
         eng = topo.engines(T.cores[0] if r else T.cores[1], core)
         return (sem, len(eng[::2] if few else eng))
 
-    def gather(out, win, lst, c0, deps, kv=32):
+    def gather(out, win, lst, c0, deps, kv=32, lo=0, hi=64):
         wait("V", deps)
-        a = done("V", g.vector.tensor_copy(T[out][:, 0:16 * kv], win.indirect(T[lst][:, c0:c0 + kv])))
+        a = done("V", g.vector.tensor_copy(T[out][:, 16 * lo:16 * kv], win.indirect(T[lst][:, c0 + lo:c0 + kv])))
         wait("S", deps)
-        b = done("S", g.scalar.activation(T[out][:, 16 * kv:1024], win.indirect(T[lst][:, c0 + kv:c0 + 64]), F.Copy))
+        b = done("S", g.scalar.activation(T[out][:, 16 * kv:16 * hi], win.indirect(T[lst][:, c0 + kv:c0 + hi]), F.Copy))
         return [a, b]
 
     compose = r in (1, 2)
@@ -98,75 +94,84 @@ def rank_program(g, core, T, topo):
     g.sync.dma_start(T.X[24:32, :], T.lit[:, 0:128]).then_inc(T.sem.ld, 16)
     g.scalar.dma_start(T.X[56:64, :], T.lit[:, 128:256]).then_inc(T.sem.ld, 16)
 
-    def iota_bl():
-        return iota(T.KBL[:, :], [[-1, 8], [0, 16]], -24, 1)
-
     dEI = iota(T.EI[:, 0:65], [[16, 65]], 0, 0)
-    d24 = iota(T.K24[:, :], [[-1, 3], [-3, 8]], 0, 1)
-    if r == 0:
-        dBL = iota_bl()
-    dSel = iota(T.KSel[:, :], [[-3, 2], [0, 16], [-6, 4]], -32, 1)
-    dPC = done("G", g.iota(T.PC[:, 0:1], [[0, 1]], 0, 1))
-    dKZ = iota(T.KZ[:, 0:143], [[1, 143]], -15, -1)
-    dQR = iota(T.QR[:, :], [[1, 16], [0, 4]], 0, 0)
+    dQN = iota(T.QN[0:1, 0:64], [[-1, 16], [0, 4]], 0, 0)
     if compose:
-        dID0 = iota(T.ID[:, 0:640], [[1, 640]], 0, 0)
+        dID = iota(T.ID[:, 0:160], [[1, 160]], 0, 0)
+    d24 = iota(T.K24[:, :], [[-1, 3], [-3, 8]], 0, 1)
+    dSel = iota(T.KSel[:, :], [[0, 16], [-6, 4]], -32, 1)
+    if r == 0:
+        dBL = iota(T.KBL[:, :], [[-1, 8], [0, 16]], -24, 1)
+    dPC = done("G", g.iota(T.PC[:, 0:1], [[0, 1]], 0, 1))
     if r:
-        dBL = iota_bl()
-    for j in range(6):
-        dZero = act(T.AB[:, 192 * j + 64:192 * j + 128], T.EI[:, 0:64], dEI, scale=0.0)
-    d1 = act(T.AS[:, 0:128], T.KSel[:, :], dSel, func=F.Abs, bias=-1.0)
-    d2 = act(T.AS[:, 128:256], T.KSel[:, :], func=F.Abs, bias=-2.0)
-    d3 = act(T.AZ[:, :], T.KZ[:, 15:143], dKZ, func=F.Abs)
-    act(T.Sel[:, 128:256], T.AS[:, 0:128], d1, func=F.Relu, bias=1.0, scale=-1.0)
-    dSelS = act(T.Sel[:, 256:384], T.AS[:, 128:256], d2, func=F.Relu, bias=1.0, scale=-1.0)
-    dI = act(T.I128[:, :], T.AZ[:, :], d3, func=F.Relu, bias=1.0, scale=-1.0)
+        dBL = iota(T.KBL[:, :], [[-1, 8], [0, 16]], -24, 1)
+    if compose:
+        dMP = iota(T.MP[:, 1024:1280], [[1, 256]], 1024, 0)
+        dMQ = iota(T.MQ[:, 1024:1280], [[1, 256]], 1024, 0)
+        dKZ = iota(T.KZ[:, 0:143], [[1, 143]], -15, -1)
+        if r == 2:
+            dMR = iota(T.MR[:, 1024:1280], [[1, 256]], 1280, 0)
+
+    for j in range(7):
+        dZero = act(T.AB[:, 192 * j:192 * j + 64], T.EI[:, 0:64], dEI, scale=0.0)
+    if compose:
+        for n in (160, 320, 640):
+            dID = act(T.ID[:, n:2 * n], T.ID[:, 0:n], dID, bias=float(n))
 
     def one_hot_bl():
         ts(T.BL[:, 0:128], T.KBL[:, :], 0.0, None, A.is_equal, None, dBL)
         return ts(T.BL[:, 128:256], T.KBL[:, :], 32.0, None, A.is_equal, None)
 
+    dSelc = []
+
+    def one_hot_sel(k):
+        ts(T.Sel[:, 128 * k:128 * k + 64], T.KSel[:, :], k + 3.0, None, A.is_equal, None, dSel)
+        dSelc.append(ts(T.Sel[:, 128 * k + 64:128 * k + 128], T.KSel[:, :], float(k), None, A.is_equal, None))
+
+    dONE = done("V", g.vector.memset(T.ONE[0:1, :], 1.0))
     vcopy(T.X16[:, 0:1], T.EI[0:64, 0:1], dEI)
     vcopy(T.F16[:, 0:1], T.EI[0:64, 0:1])
+    dQN = vcopy(T.QN[0:1, 64:128], T.QN[0:1, 0:64], dQN)
     ts(T.RS[:, 0:24], T.K24[:, :], 0.0, None, A.is_equal, None, d24)
-    ts(T.RS[:, 24:48], T.K24[:, :], 0.0, -1.0, A.is_equal, A.mult)
-    ts(T.RS[:, 48:72], T.K24[:, :], 32.0, -1.0, A.is_equal, A.mult)
+    ts(T.RS[:, 48:72], T.K24[:, :], 0.0, -1.0, A.is_equal, A.mult)
     dRS = ts(T.RS[:, 72:96], T.K24[:, :], 32.0, None, A.is_equal, None)
+    wait("V", [dRS])
+    dRS = done("V", g.vector.tensor_tensor(T.RS[:, 24:48], T.RS[:, 48:72], T.RS[:, 72:96], A.subtract))
+    one_hot_sel(0)
     if r == 0:
         dBLc = one_hot_bl()
-    dSel0 = ts(T.Sel[:, 0:128], T.KSel[:, :], 0.0, None, A.is_equal, None, dSel)
-    d = ts(T.PCa[:, 0:1], T.PC[:, 0:1], 15, None, A.bitwise_and, None, dPC)
-    d = vcopy(T.QC[:, 0:1], T.PCa[:, 0:1], d)
-    dPL = ts(T.PLC[:, :], T.EI[:, 0:64], T.QC[:, 0:1], None, A.add, None, d)
-    if compose:
-        d = ts(T.Q0[:, 0:1], T.QC[:, 0:1], 0.0, None, A.is_equal, None)
-        dZ = ts(T.Z[:, 0:143], T.KZ[:, 0:143], 0.0, T.Q0[:, 0:1], A.is_equal, A.mult, d, dKZ)
+
+    qb = [T.b2, T.b3, T.b4]
+    lb = [T.b5, T.b6, T.b7]
+    dlb = [mm(lb[k][:, 0:64], T.ONE[0:1, :], T.EI[0:1, 0:64], True, False, dONE, dEI) for k in range(3)]
+    dqb = [mm(qb[k][:, 0:128], T.ONE[0:1, :], T.QN[0:1, :], True, False, dQN) for k in range(3)]
 
     dX = vcopy(T.X16[:, 1:129], T.X[:, :], ("ld", 64))
     wait("V", [dX])
     dF = done("V", g.vector.tensor_tensor_scan(T.F16[32:56, 1:129], T.X16[32:56, 1:129], T.X16[32:56, 1:129], 0.0, A.add, A.max))
-    dC = ts(T.CI[32:56, :], T.F16[32:56, 0:128], 0.0625, -0.46875, A.mult, A.add, dF)
-    dC = ts(T.C16[32:56, :], T.CI[32:56, :], -16.0, None, A.mult, None, dC)
+    dB = ts(T.B16[32:56, :], T.F16[32:56, 0:128], -1.0, -16392.5, A.mult, A.add, dF)
+    one_hot_sel(1)
+    one_hot_sel(2)
+    d = ts(T.PCa[:, 0:1], T.PC[:, 0:1], 15, None, A.bitwise_and, None, dPC)
+    dQC = vcopy(T.QC[:, 0:1], T.PCa[:, 0:1], d)
+    if r == 0:
+        dQC = ts(T.QC[:, 1:2], T.QC[:, 0:1], -1024.0, None, A.add, None, dQC)
 
     def literals():
-        mm(T.b1[:, 0:128], T.BL[:, 0:128], T.X16[:, 1:129], True, True, dBLc)
+        mm(T.b1[:, 0:128], T.BL[:, 0:128], T.X16[:, 1:129], True, True, dBLc, dX)
         return mm(T.b1[:, 128:256], T.BL[:, 128:256], T.X16[:, 1:129], True, True)
 
-    qb = [T.b2, T.b3, T.b4]
-    lb = [T.b5, T.b6, T.b7]
-
-    def remainders(k, *deps):
+    def remainders(k):
         sel = T.Sel[32:56, 128 * k:128 * k + 128]
-        mm(qb[k][:, 0:128], T.F16[32:56, 0:128], sel, True, False, *deps)
-        return mm(qb[k][:, 0:128], T.C16[32:56, :], sel, False, True, dC)
+        mm(qb[k][:, 0:128], T.F16[32:56, 0:128], sel, False, False, dSelc[k], dF, dqb[k])
+        return mm(qb[k][:, 0:128], T.B16[32:56, :], sel, False, True, dB)
 
-    mm(T.b0[:, 32:56], T.X16[:, 1:129], T.RS[:, 0:24], True, False, dRS, dX)
-    mm(T.b0[:, 32:56], T.X16[:, 0:128], T.RS[:, 24:48], False, False)
-    mm(T.b0[:, 32:56], T.X16[:, 0:128], T.RS[:, 48:72], False, True)
     if r == 0:
         dLR = literals()
+    mm(T.b0[:, 32:56], T.X16[:, 1:129], T.RS[:, 0:24], True, False, dRS, dX)
+    mm(T.b0[:, 32:56], T.X16[:, 0:128], T.RS[:, 24:48], False, True)
     dFT = mm(T.b0[:, 0:24], T.F16[32:56, 0:128], T.RS[32:56, 72:96], True, True, dF)
-    dQ = [remainders(0, dSel0), remainders(1, dSelS)]
+    dQ = [remainders(k) for k in range(3)]
 
     tails = [("V0", 1024), ("V2", 1024), ("V5", 1024), ("V5", 1280)][r:r + 1] + [("Ya", 1024), ("Yb", 1024)]
     dT = {}
@@ -177,62 +182,53 @@ def rank_program(g, core, T, topo):
         if i == 0 and r < 3:
             send([[1, 3], [2, 3], [3]][r], b, b, c, c + 256, "rl%d" % r, False, dT[b])
 
-    if r == 0:
-        for i in range(3):
-            tail(i)
-    if compose:
-        dID = act(T.ID[:, 640:1280], T.ID[:, 0:640], dID0, bias=640.0)
-        dMP = iota(T.MP[:, 1024:1280], [[1, 256]], 1024, 0)
-        dMQ = iota(T.MQ[:, 1024:1280], [[1, 256]], 1024, 0)
-        if r == 2:
-            dMR = iota(T.MR[:, 1024:1280], [[1, 256]], 1280, 0)
+    def masks(k):
+        sg = T.Sg[:, 128 * k:128 * k + 128]
+        d = act(sg, qb[k][:, 0:128], dQ[k], func=F.Sign, bias=16399.5)
+        a = act(T.AB[:, 384 * k + 64:384 * k + 192], sg, d, func=F.Relu, scale=-1.0)
+        return a, act(T.AB[:, 384 * k + 256:384 * k + 384], sg, func=F.Relu)
 
-    def e_op(k, gd):
-        s = 8 * k + gd
-        e0 = 576 * k + 72 * gd
-        return ts(T.E[:, e0:e0 + 65], T.EI[:, 0:65], T.b0[:, s:s + 1], T.b0[:, 32 + s:33 + s], A.is_gt, A.mult, dFT)
-
-    def steps_v(k):
-        dE = [e_op(k, gd) for gd in range(4)]
-        o = 384 * k
-        tt(T.AB[:, o:o + 64], qb[k][:, 0:64], T.QR[:, :], A.is_le, dQ[k], dQR)
-        tt(T.AB[:, o + 192:o + 256], qb[k][:, 0:64], T.QR[:, :], A.is_gt)
-        tt(T.AB[:, o + 128:o + 192], qb[k][:, 64:128], T.QR[:, :], A.is_le)
-        dA = tt(T.AB[:, o + 320:o + 384], qb[k][:, 64:128], T.QR[:, :], A.is_gt)
-        return dA, dE + [e_op(k, gd) for gd in range(4, 8)]
+    def steps_e(k, gds):
+        dE = []
+        for gd in gds:
+            s = 8 * k + gd
+            e0 = 576 * k + 72 * gd
+            dE.append(ts(T.E[:, e0:e0 + 65], T.EI[:, 0:65], T.b0[:, s:s + 1], T.b0[:, 32 + s:33 + s], A.is_gt, A.mult, dFT))
+        return dE
 
     def steps_p(k, dA, dE):
-        o = 384 * k
-        mm(lb[k][:, 0:64], T.I128[:, :], T.PLC[:, :], True, False, dI, dPL)
-        for gd in range(8):
-            a, par = gd // 2, gd % 2
-            e0 = 576 * k + 72 * gd
-            out = lb[k][32 * a:32 * a + 32, 0:64]
-            s0 = o + 64 * par + a
-            mm(out, T.AB[:, s0:s0 + 125:4], T.E[:, e0 + 1:e0 + 65], False, False, dZero, dA, dE[gd])
-            dl = mm(out, T.AB[:, s0 + 192:s0 + 317:4], T.E[:, e0:e0 + 64], False, par == 1)
+        for half in range(2):
+            for gd in range(8):
+                a, par = gd // 2, gd % 2
+                e0 = 576 * k + 72 * gd + 1 - half
+                s0 = 384 * k + 128 * (1 - par) + a + 192 * half
+                dl = mm(lb[k][32 * a:32 * a + 32, 0:64], T.AB[:, s0:s0 + 125:4], T.E[:, e0:e0 + 64], False, half + par == 2,
+                        dZero, dA[half], dE[gd], dlb[k])
         return dl
 
     def take(k, dl):
-        out = T.L[:, 64 * k:64 * k + 64]
-        if r == 0 and k == 0:
-            dL.append(ts(out, lb[k][:, 0:64], -1024.0, None, A.add, None, dl))
-        else:
-            dL.append(vcopy(out, lb[k][:, 0:64], dl))
+        c = 1 if r == 0 and k == 0 else 0
+        dL.append(ts(T.L[:, 64 * k:64 * k + 64], lb[k][:, 0:64], T.QC[:, c:c + 1], None, A.add, None, dl, dQC))
         if r == 0:
             send([1, 3], "L", "L0r", 64 * k, 64 * k + 64, "rA%d" % k, False, dL[k])
         if r == 3 and k == 0:
             send([2], "L", "L9r", 0, 64, "rL9", True, dL[0])
 
     dL = []
-    dl0 = steps_p(0, *steps_v(0))
-    dQ.append(remainders(2))
-    dl1 = steps_p(1, *steps_v(1))
-    take(0, dl0)
+    if r == 0:
+        tail(0)
+    dA = [masks(k) for k in range(3)]
+    dl = [steps_p(0, dA[0], steps_e(0, range(8)))]
     if r:
         dBLc = one_hot_bl()
+    dl.append(steps_p(1, dA[1], steps_e(1, range(8))))
+    early = 2 if r else 6
+    dE = steps_e(2, range(early))
+    take(0, dl[0])
+    dE += steps_e(2, range(early, 8))
+    if r:
         dLR = literals()
-    dl2 = steps_p(2, *steps_v(2))
+    dl.append(steps_p(2, dA[2], dE))
 
     def store(k, b, deps):
         wait("Y", deps)
@@ -240,48 +236,60 @@ def rank_program(g, core, T, topo):
         cnt["st"] += 16
 
     if r == 0:
-        d = gather("Ya", T.V0[:, 1024:1280], "L", 0, [dL[0], dT["V0"]], 18)
+        tail(1)
+        d = gather("Ya", T.V0[:, 1024:1280], "L", 0, [dL[0], dT["V0"]])
         store(0, "Ya", d)
-        take(1, dl1)
-        d = gather("Yb", T.Ya[:, 0:1280], "L", 64, d + [dL[1], dT["Ya"]])
+        take(1, dl[1])
+        tail(2)
+        d = gather("Yb", T.Ya[:, 0:1280], "L", 64, d + [dL[1], dT["Ya"]], 36)
         store(1, "Yb", d)
-        take(2, dl2)
-        d = gather("V2", T.Yb[:, 0:1280], "L", 128, d + [dL[2], dT["Yb"]])
-        send([2], "V2", "V2", 0, 1024, "rV", False, *d)
+        take(2, dl[2])
+        d += [dL[2], dT["Yb"]]
+        for h in (0, 32):
+            dh = gather("V2", T.Yb[:, 0:1280], "L", 128, d, h + 16, h, h + 32)
+            send([2], "V2", "V2", 16 * h, 16 * h + 512, "rV", False, *dh)
         g.dma_start(T.y[:, 2048:3072], T.V2[0:128:16, 0:1024]).then_inc(T.sem.sc, 16)
         wait("G", [("sc", 16)])
     else:
         if compose:
-            d = gather("MP", T.ID[:, 0:1280], "L", 0, [dL[0], dID], 18)
-        take(1, dl1)
+            d = gather("MP", T.ID[:, 0:1280], "L", 0, [dL[0], dID], 28)
+        take(1, dl[1])
         tail(0)
         if compose:
-            d = gather("MQ", T.MP[:, 0:1280], "L", 64, d + [dL[1], dMP])
-        take(2, dl2)
+            d = gather("MQ", T.MP[:, 0:1280], "L", 64, d + [dL[1], dMP], 36)
+            dQ0 = ts(T.Q0[:, 0:1], T.QC[:, 0:1], 0.0, None, A.is_equal, None, dQC)
+        take(2, dl[2])
         if r == 1:
             d = gather("H16", T.MQ[:, 0:1280], "L", 128, d + [dL[2], dMQ])
         if r == 2:
             d = gather("MR", T.MQ[:, 0:1280], "L", 128, d + [dL[2], dMQ])
             d = gather("H16", T.MR[:, 0:1280], "L9r", 0, d + [dMR, arrived("rL9", True)])
         if compose:
+            dZ = ts(T.Z[:, 0:143], T.KZ[:, 0:143], 0.0, T.Q0[:, 0:1], A.is_equal, A.mult, dQ0, dKZ)
             for t in range(16):
                 dc = mm(T.b2[:, 0:64], T.Z[:, 15 - t:143 - t], T.H16[:, t:1024:16], t == 0, t == 15, dZ, *d)
+            if r == 1:
+                d = gather("V0", T.V0[:, 1024:1280], "L0r", 0, [arrived("rl0"), arrived("rA0")], 24)
             dM = vcopy(T.MU[:, :], T.b2[:, 0:64], dc)
             if r == 1:
                 send([2, 3], "MU", "M35", 0, 64, "rM1", False, dM)
             else:
                 send([3], "MU", "M69", 0, 64, "rM2", False, dM)
-        tail(1)
-        tail(2)
+        if r != 1:
+            tail(1)
+            tail(2)
         if r == 2:
-            d = [arrived("rV")]
+            d = [("rV", 2 * arrived("rV")[1])]
         else:
-            d = gather("V0", T.V0[:, 1024:1280], "L0r", 0, [arrived("rl0"), arrived("rA0")])
+            if r == 3:
+                d = gather("V0", T.V0[:, 1024:1280], "L0r", 0, [arrived("rl0"), arrived("rA0")])
             dV1 = act(T.V1[:, 1024:1280], T.V0[:, 1024:1280])
-            d = gather("V1", T.V0[:, 0:1280], "L0r", 64, d + [arrived("rA1")], 36)
+            d = gather("V1", T.V0[:, 0:1280], "L0r", 64, d + [arrived("rA1")], 38)
             d = gather("V2", T.V1[:, 0:1280], "L0r", 128, d + [arrived("rA2"), dV1])
         if r == 1:
-            d = gather("Ya", T.V2[:, 0:1280], "L", 0, d + [dT["V2"], dL[0]])
+            tail(1)
+            d = gather("Ya", T.V2[:, 0:1280], "L", 0, d + [dT["V2"], dL[0]], 38)
+            tail(2)
         else:
             d = gather("V5", T.V2[:, 0:1280], "M35", 0, d + [arrived("rl1"), arrived("rM1")])
             if r == 2:

from concourse.bass import DstId, RemoteDMATransfer
from concourse.mybir import AluOpType as A, ActivationFunctionType as F


def _bufs():
    b = {}
    for dtype, names in (("int32", "X 64 128, PC 128 4, PCa 128 4"),
                         ("uint16", "L 128 192, L0r 128 192, L9r 128 64, MU 128 64, M35 128 64, M69 128 64"),
                         ("float16", "X16 64 136, F16 64 136, B16 64 128, Z 128 144, RS 64 96, BL 64 256, Sel 64 384, "
                                     "Sg 128 384, AB 128 1216, E 128 1728, H16 128 1024"),
                         ("bfloat16", "EI 128 72, QN 128 128, ONE 128 128, V0 128 1280, V1 128 1280, V2 128 1280, V5 128 1536"),
                         ("float32", "K24 64 24, KBL 64 128, KSel 64 64, QC 128 4, Q0 128 4, KZ 128 144, "
                                     "ID 128 1280, MP 128 1280, MQ 128 1280, MR 128 1280, "
                                     "Ya 128 1280, Yb 128 1280, Yc 128 1024")):
        for s in names.split(","):
            n, p, c = s.split()
            b[n] = ("sbuf", [int(p), int(c)], dtype)
    for i in range(8):
        b["b%d" % i] = ("psum", [128, 512], "float32")
    return b


SCRATCH = _bufs()
SEMAPHORES = ["sV", "sS", "sP", "sG", "ld", "st", "sc", "lo", "rl0", "rl1", "rl2", "rA0", "rA1", "rA2", "rV", "rM1", "rM2", "rL9"]


def rank_program(g, core, T, topo):
    r = T.rank_of(core)
    if r is None:
        return
    q = {"V": g.vector, "S": g.scalar, "P": g.tensor, "G": g, "Y": g.sync}
    cnt = {"V": 0, "S": 0, "P": 0, "G": 0, "lo": 0, "st": 0}
    seen = {e: {} for e in q}

    def wait(e, deps):
        for s, n in deps:
            if seen[e].get(s, 0) < n:
                q[e].wait_ge(T.sem[s], n)
                seen[e][s] = n

    def done(e, ins):
        cnt[e] += 1
        ins.then_inc(T.sem["s" + e], 1)
        return ("s" + e, cnt[e])

    def iota(out, pattern, base, cm):
        return done("G", g.iota(out, pattern, base, cm, allow_small_or_imprecise_dtypes=True))

    def vcopy(out, in_, *deps):
        wait("V", deps)
        return done("V", g.vector.tensor_copy(out, in_))

    def ts(out, in0, s1, s2, op0, op1, *deps):
        wait("V", deps)
        if op1 is None:
            return done("V", g.vector.tensor_scalar(out, in0, s1, None, op0))
        return done("V", g.vector.tensor_scalar(out, in0, s1, s2, op0, op1))

    def act(out, in_, *deps, func=F.Identity, bias=0.0, scale=1.0):
        wait("S", deps)
        return done("S", g.scalar.activation(out, in_, func, bias=bias, scale=scale))

    def mm(out, lhsT, rhs, start, stop, *deps):
        wait("P", deps)
        return done("P", g.tensor.matmul(out, lhsT, rhs, start, stop))

    def send(dsts, src, dst, c0, c1, sem, few, *deps):
        wait("G", deps)
        cores = [T.cores[d] for d in dsts]
        eng = topo.engines(core, cores[0])
        if few:
            eng = eng[::2]
        at = [topo.addr(c) for c in cores]
        g.remote_dma_fused([RemoteDMATransfer(dst_ids=[DstId(rid=a[0], pnc=a[1]) for a in at],
                                              dma_engine_mask=sum(1 << e for e in eng), remote_sem=T.sem[sem],
                                              srcs=[T[src][:, c0:c1]], dsts=[T[dst][:, c0:c1] for c in cores])],
                           local_sem=T.sem.lo)
        cnt["lo"] += len(eng)

    def arrived(sem, few=False):
        eng = topo.engines(T.cores[0] if r else T.cores[1], core)
        return (sem, len(eng[::2] if few else eng))

    def gather(out, win, lst, c0, deps, kv=32, lo=0, hi=64):
        wait("V", deps)
        a = done("V", g.vector.tensor_copy(T[out][:, 16 * lo:16 * kv], win.indirect(T[lst][:, c0 + lo:c0 + kv])))
        wait("S", deps)
        b = done("S", g.scalar.activation(T[out][:, 16 * kv:16 * hi], win.indirect(T[lst][:, c0 + kv:c0 + hi]), F.Copy))
        return [a, b]

    compose = r in (1, 2)
    g.sync.dma_start(T.X[32:56, :], T.ln[:]).then_inc(T.sem.ld, 16)
    g.scalar.dma_start(T.X[0:24, :], T.frm[:]).then_inc(T.sem.ld, 16)
    g.sync.dma_start(T.X[24:32, :], T.lit[:, 0:128]).then_inc(T.sem.ld, 16)
    g.scalar.dma_start(T.X[56:64, :], T.lit[:, 128:256]).then_inc(T.sem.ld, 16)

    dEI = iota(T.EI[:, 0:65], [[16, 65]], 0, 0)
    dQN = iota(T.QN[0:1, 0:64], [[-1, 16], [0, 4]], 0, 0)
    if compose:
        dID = iota(T.ID[:, 0:160], [[1, 160]], 0, 0)
    d24 = iota(T.K24[:, :], [[-1, 3], [-3, 8]], 0, 1)
    dSel = iota(T.KSel[:, :], [[0, 16], [-6, 4]], -32, 1)
    if r == 0:
        dBL = iota(T.KBL[:, :], [[-1, 8], [0, 16]], -24, 1)
    dPC = done("G", g.iota(T.PC[:, 0:1], [[0, 1]], 0, 1))
    if r:
        dBL = iota(T.KBL[:, :], [[-1, 8], [0, 16]], -24, 1)
    if compose:
        dMP = iota(T.MP[:, 1024:1280], [[1, 256]], 1024, 0)
        dMQ = iota(T.MQ[:, 1024:1280], [[1, 256]], 1024, 0)
        dKZ = iota(T.KZ[:, 0:143], [[1, 143]], -15, -1)
        if r == 2:
            dMR = iota(T.MR[:, 1024:1280], [[1, 256]], 1280, 0)

    for j in range(7):
        dZero = act(T.AB[:, 192 * j:192 * j + 64], T.EI[:, 0:64], dEI, scale=0.0)
    if compose:
        for n in (160, 320, 640):
            dID = act(T.ID[:, n:2 * n], T.ID[:, 0:n], dID, bias=float(n))

    def one_hot_bl():
        ts(T.BL[:, 0:128], T.KBL[:, :], 0.0, None, A.is_equal, None, dBL)
        return ts(T.BL[:, 128:256], T.KBL[:, :], 32.0, None, A.is_equal, None)

    dSelc = []

    def one_hot_sel(k):
        ts(T.Sel[:, 128 * k:128 * k + 64], T.KSel[:, :], k + 3.0, None, A.is_equal, None, dSel)
        dSelc.append(ts(T.Sel[:, 128 * k + 64:128 * k + 128], T.KSel[:, :], float(k), None, A.is_equal, None))

    dONE = done("V", g.vector.memset(T.ONE[0:1, :], 1.0))
    vcopy(T.X16[:, 0:1], T.EI[0:64, 0:1], dEI)
    vcopy(T.F16[:, 0:1], T.EI[0:64, 0:1])
    dQN = vcopy(T.QN[0:1, 64:128], T.QN[0:1, 0:64], dQN)
    ts(T.RS[:, 0:24], T.K24[:, :], 0.0, None, A.is_equal, None, d24)
    ts(T.RS[:, 48:72], T.K24[:, :], 0.0, -1.0, A.is_equal, A.mult)
    dRS = ts(T.RS[:, 72:96], T.K24[:, :], 32.0, None, A.is_equal, None)
    wait("V", [dRS])
    dRS = done("V", g.vector.tensor_tensor(T.RS[:, 24:48], T.RS[:, 48:72], T.RS[:, 72:96], A.subtract))
    one_hot_sel(0)
    if r == 0:
        dBLc = one_hot_bl()

    qb = [T.b2, T.b3, T.b4]
    lb = [T.b5, T.b6, T.b7]
    dlb = [mm(lb[k][:, 0:64], T.ONE[0:1, :], T.EI[0:1, 0:64], True, False, dONE, dEI) for k in range(3)]
    dqb = [mm(qb[k][:, 0:128], T.ONE[0:1, :], T.QN[0:1, :], True, False, dQN) for k in range(3)]

    dX = vcopy(T.X16[:, 1:129], T.X[:, :], ("ld", 64))
    wait("V", [dX])
    dF = done("V", g.vector.tensor_tensor_scan(T.F16[32:56, 1:129], T.X16[32:56, 1:129], T.X16[32:56, 1:129], 0.0, A.add, A.max))
    dB = ts(T.B16[32:56, :], T.F16[32:56, 0:128], -1.0, -16392.5, A.mult, A.add, dF)
    one_hot_sel(1)
    one_hot_sel(2)
    d = ts(T.PCa[:, 0:1], T.PC[:, 0:1], 15, None, A.bitwise_and, None, dPC)
    dQC = vcopy(T.QC[:, 0:1], T.PCa[:, 0:1], d)
    if r == 0:
        dQC = ts(T.QC[:, 1:2], T.QC[:, 0:1], -1024.0, None, A.add, None, dQC)

    def literals():
        mm(T.b1[:, 0:128], T.BL[:, 0:128], T.X16[:, 1:129], True, True, dBLc, dX)
        return mm(T.b1[:, 128:256], T.BL[:, 128:256], T.X16[:, 1:129], True, True)

    def remainders(k):
        sel = T.Sel[32:56, 128 * k:128 * k + 128]
        mm(qb[k][:, 0:128], T.F16[32:56, 0:128], sel, False, False, dSelc[k], dF, dqb[k])
        return mm(qb[k][:, 0:128], T.B16[32:56, :], sel, False, True, dB)

    if r == 0:
        dLR = literals()
    mm(T.b0[:, 32:56], T.X16[:, 1:129], T.RS[:, 0:24], True, False, dRS, dX)
    mm(T.b0[:, 32:56], T.X16[:, 0:128], T.RS[:, 24:48], False, True)
    dFT = mm(T.b0[:, 0:24], T.F16[32:56, 0:128], T.RS[32:56, 72:96], True, True, dF)
    dQ = [remainders(k) for k in range(3)]

    tails = [("V0", 1024), ("V2", 1024), ("V5", 1024), ("V5", 1280)][r:r + 1] + [("Ya", 1024), ("Yb", 1024)]
    dT = {}

    def tail(i):
        b, c = tails[i]
        dT[b] = act(T[b][:, c:c + 256], T.b1[:, 0:256], dLR)
        if i == 0 and r < 3:
            send([[1, 3], [2, 3], [3]][r], b, b, c, c + 256, "rl%d" % r, False, dT[b])

    def masks(k):
        sg = T.Sg[:, 128 * k:128 * k + 128]
        d = act(sg, qb[k][:, 0:128], dQ[k], func=F.Sign, bias=16399.5)
        a = act(T.AB[:, 384 * k + 64:384 * k + 192], sg, d, func=F.Relu, scale=-1.0)
        return a, act(T.AB[:, 384 * k + 256:384 * k + 384], sg, func=F.Relu)

    def steps_e(k, gds):
        dE = []
        for gd in gds:
            s = 8 * k + gd
            e0 = 576 * k + 72 * gd
            dE.append(ts(T.E[:, e0:e0 + 65], T.EI[:, 0:65], T.b0[:, s:s + 1], T.b0[:, 32 + s:33 + s], A.is_gt, A.mult, dFT))
        return dE

    def steps_p(k, dA, dE):
        for half in range(2):
            for gd in range(8):
                a, par = gd // 2, gd % 2
                e0 = 576 * k + 72 * gd + 1 - half
                s0 = 384 * k + 128 * (1 - par) + a + 192 * half
                dl = mm(lb[k][32 * a:32 * a + 32, 0:64], T.AB[:, s0:s0 + 125:4], T.E[:, e0:e0 + 64], False, half + par == 2,
                        dZero, dA[half], dE[gd], dlb[k])
        return dl

    def take(k, dl):
        c = 1 if r == 0 and k == 0 else 0
        dL.append(ts(T.L[:, 64 * k:64 * k + 64], lb[k][:, 0:64], T.QC[:, c:c + 1], None, A.add, None, dl, dQC))
        if r == 0:
            send([1, 3], "L", "L0r", 64 * k, 64 * k + 64, "rA%d" % k, False, dL[k])
        if r == 3 and k == 0:
            send([2], "L", "L9r", 0, 64, "rL9", True, dL[0])

    dL = []
    if r == 0:
        tail(0)
    dA = [masks(k) for k in range(3)]
    dl = [steps_p(0, dA[0], steps_e(0, range(8)))]
    if r:
        dBLc = one_hot_bl()
    dl.append(steps_p(1, dA[1], steps_e(1, range(8))))
    early = 2 if r else 6
    dE = steps_e(2, range(early))
    take(0, dl[0])
    dE += steps_e(2, range(early, 8))
    if r:
        dLR = literals()
    dl.append(steps_p(2, dA[2], dE))

    def store(k, b, deps):
        wait("Y", deps)
        g.sync.dma_start(T.y[:, 1024 * k:1024 * k + 1024], T[b][0:128:16, 0:1024]).then_inc(T.sem.st, 16)
        cnt["st"] += 16

    if r == 0:
        tail(1)
        d = gather("Ya", T.V0[:, 1024:1280], "L", 0, [dL[0], dT["V0"]])
        store(0, "Ya", d)
        take(1, dl[1])
        tail(2)
        d = gather("Yb", T.Ya[:, 0:1280], "L", 64, d + [dL[1], dT["Ya"]], 36)
        store(1, "Yb", d)
        take(2, dl[2])
        d += [dL[2], dT["Yb"]]
        for h in (0, 32):
            dh = gather("V2", T.Yb[:, 0:1280], "L", 128, d, h + 16, h, h + 32)
            send([2], "V2", "V2", 16 * h, 16 * h + 512, "rV", False, *dh)
        g.dma_start(T.y[:, 2048:3072], T.V2[0:128:16, 0:1024]).then_inc(T.sem.sc, 16)
        wait("G", [("sc", 16)])
    else:
        if compose:
            d = gather("MP", T.ID[:, 0:1280], "L", 0, [dL[0], dID], 28)
        take(1, dl[1])
        tail(0)
        if compose:
            d = gather("MQ", T.MP[:, 0:1280], "L", 64, d + [dL[1], dMP], 36)
            dQ0 = ts(T.Q0[:, 0:1], T.QC[:, 0:1], 0.0, None, A.is_equal, None, dQC)
        take(2, dl[2])
        if r == 1:
            d = gather("H16", T.MQ[:, 0:1280], "L", 128, d + [dL[2], dMQ])
        if r == 2:
            d = gather("MR", T.MQ[:, 0:1280], "L", 128, d + [dL[2], dMQ])
            d = gather("H16", T.MR[:, 0:1280], "L9r", 0, d + [dMR, arrived("rL9", True)])
        if compose:
            dZ = ts(T.Z[:, 0:143], T.KZ[:, 0:143], 0.0, T.Q0[:, 0:1], A.is_equal, A.mult, dQ0, dKZ)
            for t in range(16):
                dc = mm(T.b2[:, 0:64], T.Z[:, 15 - t:143 - t], T.H16[:, t:1024:16], t == 0, t == 15, dZ, *d)
            if r == 1:
                d = gather("V0", T.V0[:, 1024:1280], "L0r", 0, [arrived("rl0"), arrived("rA0")], 24)
            dM = vcopy(T.MU[:, :], T.b2[:, 0:64], dc)
            if r == 1:
                send([2, 3], "MU", "M35", 0, 64, "rM1", False, dM)
            else:
                send([3], "MU", "M69", 0, 64, "rM2", False, dM)
        if r != 1:
            tail(1)
            tail(2)
        if r == 2:
            d = [("rV", 2 * arrived("rV")[1])]
        else:
            if r == 3:
                d = gather("V0", T.V0[:, 1024:1280], "L0r", 0, [arrived("rl0"), arrived("rA0")])
            dV1 = act(T.V1[:, 1024:1280], T.V0[:, 1024:1280])
            d = gather("V1", T.V0[:, 0:1280], "L0r", 64, d + [arrived("rA1")], 38)
            d = gather("V2", T.V1[:, 0:1280], "L0r", 128, d + [arrived("rA2"), dV1])
        if r == 1:
            tail(1)
            d = gather("Ya", T.V2[:, 0:1280], "L", 0, d + [dT["V2"], dL[0]], 38)
            tail(2)
        else:
            d = gather("V5", T.V2[:, 0:1280], "M35", 0, d + [arrived("rl1"), arrived("rM1")])
            if r == 2:
                d = gather("Ya", T.V5[:, 0:1280], "L", 0, d + [dT["V5"], dL[0]])
            else:
                d = gather("Ya", T.V5[:, 0:1536], "M69", 0, d + [dT["V5"], arrived("rl2"), arrived("rM2")])
        store(0, "Ya", d)
        d = gather("Yb", T.Ya[:, 0:1280], "L", 64, d + [dT["Ya"], dL[1]])
        store(1, "Yb", d)
        d = gather("Yc", T.Yb[:, 0:1280], "L", 128, d + [dT["Yb"], dL[2]])
        wait("Y", d[:1])
        g.sync.dma_start(T.y[:, 2048:2560], T.Yc[0:128:16, 0:512]).then_inc(T.sem.st, 16)
        wait("S", d[1:])
        g.scalar.dma_start(T.y[:, 2560:3072], T.Yc[0:128:16, 512:1024]).then_inc(T.sem.st, 16)
        cnt["st"] += 32
    wait("Y", [("st", cnt["st"])])
    wait("G", [("sV", cnt["V"]), ("sS", cnt["S"]), ("sP", cnt["P"]), ("sG", cnt["G"]), ("lo", cnt["lo"])])
